import numpy as np
import ml_dtypes


def mxq(x, axis, fmt="e4m3"):
    dtype, down = {"e4m3": (ml_dtypes.float8_e4m3fn, 7), "e5m2": (ml_dtypes.float8_e5m2, 14)}[fmt]
    v = np.moveaxis(np.asarray(x, np.float32).astype(ml_dtypes.bfloat16).astype(np.float64), axis, -1)
    blocks = v.reshape(v.shape[:-1] + (-1, 32))
    amax = np.abs(blocks).max(-1, keepdims=True)
    byte = np.maximum(np.where(amax > 0, np.frexp(amax)[1] - 1 + 127, 0) - down, 1)
    scale = np.exp2(byte - 127.0)
    codes = (blocks / scale).astype(np.float32).astype(dtype).astype(np.float64)
    return np.moveaxis((codes * scale).reshape(v.shape), -1, axis)


WIDE = False


def mx_kscale(k):
    if not WIDE:
        return np.ones(k)
    levels = np.array([10, -10, 5, -5, 0])
    if k % 512:
        return np.exp2(np.random.permutation(np.resize(levels, k // 32))).repeat(32)
    a = np.empty((k // 512, 16))
    for p in range(k // 512):
        a[p, :8] = np.random.permutation(np.resize(levels, 8))
        for g in range(8):
            far = levels[np.abs(levels - a[p, g]) >= 10]
            a[p, g + 8] = far[np.random.randint(len(far))]
    return np.exp2(a.ravel()).repeat(32)


def f64(x):
    return np.asarray(x).astype(np.float64)


def striped(idx):
    return np.tile(idx.reshape(-1, 16).T, (8, 1)).astype(np.uint16)


def unstriped(offs):
    return offs[:16].T.reshape(-1).astype(np.int64)


E2M1 = np.array([0.0, 0.5, 1.0, 1.5, 2.0, 3.0, 4.0, 6.0, -0.0, -0.5, -1.0, -1.5, -2.0, -3.0, -4.0, -6.0])


def pack_weight(w, fmt):
    k, n = w.shape
    w = f64(np.asarray(w, np.float32).astype(ml_dtypes.bfloat16)).reshape(k // 32, 32, n)
    amax = np.abs(w).max(1)
    if fmt == "e4m3":
        byte = np.frexp(amax)[1] - 1 + 127 - 7
    else:
        mant, ex = np.frexp(amax / 6.0)
        byte = np.where(mant > 0.5, ex, ex - 1) + 127
    byte = np.clip(np.where(amax > 0, byte, 1), 1, 254)
    scaled = (w * np.exp2(127.0 - byte)[:, None, :]).reshape(k, n).astype(np.float32)
    by_word = np.ascontiguousarray(scaled.reshape(k // 512, 128, 4, n).transpose(0, 1, 3, 2))
    if fmt == "e4m3":
        words = by_word.astype(ml_dtypes.float8_e4m3fn).view(np.uint8)
    else:
        c = by_word.astype(ml_dtypes.float4_e2m1fn).view(np.uint8) & 0xF
        words = (c[..., 0::2] | (c[..., 1::2] << 4)).reshape(k // 512, 128, 2 * n)
    return np.ascontiguousarray(words), np.ascontiguousarray(byte.astype(np.uint8).reshape(k // 512, 16, n))


def unpack_weight(words, scales, fmt):
    g, _, n = scales.shape
    words = np.ascontiguousarray(words).reshape(g, 128, n, -1)
    if fmt == "e4m3":
        vals = words.view(ml_dtypes.float8_e4m3fn).astype(np.float64)
    else:
        nib = np.empty((g, 128, n, 4), np.uint8)
        nib[..., 0::2] = words & 0xF
        nib[..., 1::2] = words >> 4
        vals = E2M1[nib]
    vals = vals * np.repeat(np.exp2(scales.astype(np.float64) - 127.0), 8, axis=1)[..., None]
    return vals.transpose(0, 1, 3, 2).reshape(g * 512, n)


def gelu(v):
    return 0.5 * v * (1.0 + np.tanh(np.sqrt(2.0 / np.pi) * (v + 0.044715 * v**3)))


def twice(P):
    return np.random.permutation(np.repeat(np.arange(P), 2))


K, T, S, P, H = 1024, 2048, 1024, 512, 1024

def setup_inputs():
    n = np.random.standard_normal
    s = mx_kscale(K)[:, None]
    u = mx_kscale(H)[:, None]
    d = {}
    d["tab_words"], d["tab_scales"] = pack_weight(n((K, T)) * s, "e4m3")
    d["offs"] = striped(np.random.permutation(T)[:S])
    d["pos1"] = striped(np.random.permutation(S)[:P])
    d["pos2"] = striped(np.random.permutation(S)[:P])
    d["pos3"] = striped(twice(P))
    d["w1"] = (n((K, H)) / s * u.T / K ** 0.5).astype(np.float32)
    d["w4_words"], d["w4_scales"] = pack_weight(n((K, H)) / s * u.T / K ** 0.5, "e2m1")
    d["w2"] = (1.3 * n((H, H)) / u / H ** 0.5).astype(np.float32)
    d["gp"] = np.exp(0.4 * n(H)).astype(np.float32)
    d["gs"] = (2.5 * np.exp(0.3 * n(H)) / u[:, 0]).astype(np.float32)
    return d

def reference(tab_words, tab_scales, offs, pos1, pos2, pos3, w1, w4_words, w4_scales, w2, gp, gs):
    v = unpack_weight(tab_words, tab_scales, "e4m3")[:, unstriped(offs)]
    w4 = unpack_weight(w4_words, w4_scales, "e2m1")
    a = mxq(f64(w1), 0, "e4m3").T @ v
    b = w4.T @ v
    h = np.maximum(a, b)
    hg = f64(gp)[:, None] * h
    z = hg[:, unstriped(pos1)] + hg[:, unstriped(pos2)]
    y = mxq(f64(w2), 0, "e4m3").T @ mxq(z, 0, "e4m3")
    yr = y[:, unstriped(pos3)]
    sg = 1.0 / (1.0 + np.exp(-yr))
    return f64(gs)[:, None] * h * sg + yr

@@ -1,0 +1,290 @@
+from contextlib import ExitStack
+
+import concourse.mybir as mybir
+from concourse.masks import make_identity
+
+K, T, S, E, H = 1024, 2048, 1024, 512, 1024
+FLOPS = 2 * (2 * K * H * S + H * H * E)
+
+F32 = mybir.dt.float32
+BF16 = mybir.dt.bfloat16
+I32 = mybir.dt.int32
+U32 = mybir.dt.uint32
+U16 = mybir.dt.uint16
+U8 = mybir.dt.uint8
+FP8X4 = mybir.dt.float8_e4m3fn_x4
+FP4X4 = mybir.dt.float4_e2m1fn_x4
+ALU = mybir.AluOpType
+ACT = mybir.ActivationFunctionType
+
+P = 128
+PACK = 4
+PASS = P * PACK
+BANK = 512
+PASSES = K // PASS
+TILES = H // P
+
+
+def tile_list_sleep_episode_stager_kernel(
+    tc, tab_words, tab_scales, offs, pos1, pos2, pos3, w1, w4_words, w4_scales, w2, gp, gs, out
+):
+    nc = tc.nc
+    with ExitStack() as ctx:
+        keep = ctx.enter_context(tc.tile_pool(name="keep", bufs=1))
+        ring = ctx.enter_context(tc.tile_pool(name="ring", bufs=2))
+        psum = ctx.enter_context(tc.psum_pool(name="psum", bufs=8))
+
+        def held(shape, dtype, name):
+            return keep.tile(shape, dtype, name=name, align_bytes=64)
+
+        offs_t = held([P, S // 16], U16, "offs_t")
+        pos1_t = held([P, E // 16], U16, "pos1_t")
+        pos2_t = held([P, E // 16], U16, "pos2_t")
+        pos3_t = held([P, S // 16], U16, "pos3_t")
+        table = [held([P, T], U32, f"table{a}") for a in range(PASSES)]
+        table_sc = held([P, T], U8, "table_sc")
+        table_sc_rows = held([P, T], U8, "table_sc_rows")
+        v = [[held([P, BANK], U32, f"v{a}{u}") for u in range(2)] for a in range(PASSES)]
+        v_sc = held([P, S], U8, "v_sc")
+        v_sc1 = held([P, S], U8, "v_sc1")
+        w4_raw = held([P, PASSES * 2 * H], U8, "w4_raw")
+        w4 = held([P, PASSES * 2 * H], U8, "w4")
+        w4_sc_raw = held([P, PASSES * H], U8, "w4_sc_raw")
+        w4_sc = held([P, PASSES * H], U8, "w4_sc")
+        gains_rows = held([P, P], F32, "gains_rows")
+        ident = held([P, P], F32, "ident")
+        gains = held([P, 2 * TILES], F32, "gains")
+        h = [held([P, S], F32, f"h{i}") for i in range(TILES)]
+        ya = [held([P, E + S], F32, f"ya{i}") for i in range(4)]
+        z = [held([P, E * PACK], BF16, f"z{b}") for b in range(2)]
+        z_q = [held([P, E], U32, f"z_q{b}") for b in range(2)]
+        z_sc = [held([P, E], U8, f"z_sc{b}") for b in range(2)]
+
+        nc.vector.memset(table_sc[:].bitcast(I32), 0)
+        nc.vector.memset(w4_sc_raw[:].bitcast(I32), 0)
+        nc.vector.memset(v_sc1[:].bitcast(I32), 0)
+        nc.vector.memset(gains_rows[:], 0.0)
+        make_identity(nc, ident[:])
+
+        def load_table(a):
+            nc.sync.dma_start(
+                out=table[a][:].bitcast(I32), in_=tab_words[a].rearrange("p n i -> p (n i)").bitcast(I32)
+            )
+
+        def load_w1(a, b):
+            raw = ring.tile([P, PACK, PASS], F32, name="raw", bufs=5)
+            rows = w1[a * PASS : (a + 1) * PASS, b * PASS : (b + 1) * PASS]
+            nc.sync.dma_start(out=raw[:], in_=rows.rearrange("(p j) c -> p j c", j=PACK))
+            return raw
+
+        def load_w2(b, c):
+            raw = ring.tile([P, PACK, PASS], F32, name="raw", bufs=5)
+            rows = w2[b * PASS : (b + 1) * PASS, c * PASS : (c + 1) * PASS]
+            rows = rows.rearrange("(g t i) n -> t g i n", t=PACK, i=8)
+            for t in range(PACK):
+                nc.sync.dma_start(out=raw[:, t, :], in_=rows[t])
+            return raw
+
+        def quantise_weight(raw, name, by_tile, grouped=None):
+            if grouped is None:
+                grouped = ring.tile([P, PASS * PACK], BF16, name="grouped", bufs=3, align_bytes=64)
+            codes = held([P, PASS], U32, name + "_q")
+            scales = held([P, PASS], U8, name + "_sc")
+            src = raw[:].rearrange("p j (g t u i) -> p t g u j i", t=PACK, u=2, i=4)
+            dst = grouped[:].rearrange("p (t g u i j) -> p t g u j i", t=PACK, u=2, i=4, j=PACK)
+            for t in range(PACK):
+                nc.scalar.copy(out=dst[:, t], in_=src[:, t])
+                if by_tile:
+                    nc.vector.quantize_mx(
+                        out=codes[:, t * P : (t + 1) * P].bitcast(FP8X4),
+                        scales=scales[:, t * P : (t + 1) * P],
+                        in_=grouped[:, t * PASS : (t + 1) * PASS],
+                    )
+            if not by_tile:
+                nc.vector.quantize_mx(out=codes[:].bitcast(FP8X4), scales=scales[:], in_=grouped[:])
+            return codes, scales
+
+        nc.sync.dma_start(offs_t[:], offs)
+        for q in range(4):
+            nc.sync.dma_start(
+                out=table_sc_rows[32 * q : 32 * q + 8, :].bitcast(I32),
+                in_=tab_scales[:, 4 * q : 4 * q + 4, :].bitcast(I32),
+            )
+        load_table(0)
+        w1_raw = {(0, 0): load_w1(0, 0)}
+        load_table(1)
+        nc.sync.dma_start(
+            out=w4_raw[:].bitcast(I32).rearrange("p (a c) -> p a c", a=PASSES),
+            in_=w4_words.bitcast(I32).rearrange("a p c -> p a c"),
+        )
+        for q in range(4):
+            nc.sync.dma_start(
+                out=w4_sc_raw[32 * q : 32 * q + 4, :].bitcast(I32).rearrange("r (a c) -> r a c", a=PASSES),
+                in_=w4_scales[:, 4 * q : 4 * q + 4, :].bitcast(I32).rearrange("a r c -> r a c"),
+            )
+        w1_raw[1, 0] = load_w1(1, 0)
+        nc.sync.dma_start(pos1_t[:], pos1)
+        nc.sync.dma_start(pos2_t[:], pos2)
+        for n, vec in enumerate((gp, gs)):
+            for b in range(2):
+                row = n * TILES + b * PACK
+                nc.sync.dma_start(
+                    out=gains_rows[row : row + PACK, :].rearrange("t (g i) -> t g i", i=8),
+                    in_=vec[b * PASS : (b + 1) * PASS].rearrange("(g t i) -> t g i", t=PACK, i=8),
+                )
+        w1_raw[0, 1] = load_w1(0, 1)
+        w1_raw[1, 1] = load_w1(1, 1)
+        nc.sync.dma_start(pos3_t[:], pos3)
+
+        for q in range(4):
+            rows = slice(32 * q, 32 * q + 8)
+            nc.vector.tensor_copy(out=table_sc[rows, :].bitcast(I32), in_=table_sc_rows[rows, :].bitcast(I32))
+        nc.vector.tensor_copy(out=v_sc[:], in_=table_sc[:].indirect(offs_t[:]))
+        for q in range(4):
+            nc.scalar.dma_start(
+                out=v_sc1[32 * q : 32 * q + 4, :].bitcast(I32), in_=v_sc[32 * q + 4 : 32 * q + 8, :].bitcast(I32)
+            )
+
+        def gather_table(a):
+            for u in range(2):
+                nc.vector.tensor_copy(out=v[a][u][:], in_=table[a][:].indirect(offs_t[:, 32 * u : 32 * (u + 1)]))
+
+        w1_q = {}
+        gather_table(0)
+        w1_q[0, 0] = quantise_weight(w1_raw[0, 0], "w1_00", True)
+        gather_table(1)
+        for dst, src, words in ((w4, w4_raw, 4), (w4_sc, w4_sc_raw, 2)):
+            nc.vector.tensor_copy(
+                out=dst[:].bitcast(I32).rearrange("p (s t g w) -> p s t g w", t=PACK, g=16, w=words),
+                in_=src[:].bitcast(I32).rearrange("p (s g t w) -> p s t g w", t=PACK, g=16, w=words),
+            )
+        w1_q[1, 0] = quantise_weight(w1_raw[1, 0], "w1_10", True)
+
+        def turn_gains():
+            turned = psum.tile([P, BANK], F32, name="acc")
+            nc.tensor.transpose(turned[:, 0:P], gains_rows[:], ident[:])
+            nc.scalar.copy(out=gains[:], in_=turned[:, 0 : 2 * TILES])
+
+        def first_stage(i, u):
+            b, t = divmod(i, PACK)
+            cols = slice(u * BANK, (u + 1) * BANK)
+            acc_a = psum.tile([P, BANK], F32, name="acc")
+            for a in range(PASSES):
+                codes, scales = w1_q[a, b]
+                nc.tensor.matmul_mx(
+                    out=acc_a[:],
+                    lhsT=codes[:, t * P : (t + 1) * P].bitcast(FP8X4),
+                    lhsT_scale=scales[:, t * P : (t + 1) * P],
+                    rhs=v[a][u][:].bitcast(FP8X4),
+                    rhs_scale=v_sc[4 * a : P, cols],
+                    start=(a == 0),
+                    stop=(a == PASSES - 1),
+                )
+            acc_b = psum.tile([P, BANK], F32, name="acc")
+            for a in range(PASSES):
+                first = a * H + i * P
+                nc.tensor.matmul_mx(
+                    out=acc_b[:],
+                    lhsT=w4[:, 2 * first : 2 * (first + P)].bitcast(FP4X4),
+                    lhsT_scale=w4_sc[:, first : first + P],
+                    rhs=v[a][u][:].bitcast(FP8X4),
+                    rhs_scale=(v_sc, v_sc1)[a][:, cols],
+                    start=(a == 0),
+                    stop=(a == PASSES - 1),
+                )
+            a_sb = ya[i % 4][:, E + u * BANK : E + (u + 1) * BANK]
+            nc.scalar.copy(out=a_sb, in_=acc_a[:])
+            nc.vector.tensor_tensor(out=h[i][:, cols], in0=acc_b[:], in1=a_sb, op=ALU.max)
+
+        def pick_first(i):
+            picked = ring.tile([P, E], F32, name="picked")
+            nc.vector.tensor_copy(out=picked[:], in_=h[i][:].indirect(pos1_t[:]))
+            return picked
+
+        def join_pair(i, picked):
+            b, t = divmod(i, PACK)
+            pair = ring.tile([P, E], F32, name="pair", bufs=3)
+            nc.vector.tensor_tensor(out=pair[:], in0=h[i][:].indirect(pos2_t[:]), in1=picked[:], op=ALU.add)
+            nc.scalar.activation(
+                out=z[b][:].rearrange("p (m t) -> p t m", t=PACK)[:, t, :],
+                in_=pair[:],
+                func=ACT.Copy,
+                scale=gains[:, i : i + 1],
+            )
+            if t == PACK - 1:
+                nc.vector.quantize_mx(out=z_q[b][:].bitcast(FP8X4), scales=z_sc[b][:], in_=z[b][:])
+
+        w2_q = {}
+        later = [
+            ("w1", 0, 1), ("w1", 1, 1), ("w2", 0, 0), ("w2", 1, 0),
+        ]
+        for i in range(TILES + 1):
+            if i < TILES:
+                first_stage(i, 0)
+            if i > 0:
+                picked = pick_first(i - 1)
+            if i < TILES:
+                first_stage(i, 1)
+            if i == 0:
+                turn_gains()
+            if i > 0:
+                join_pair(i - 1, picked)
+            if i < len(later):
+                kind, a, b = later[i]
+                if kind == "w1":
+                    w1_q[a, b] = quantise_weight(w1_raw[a, b], f"w1_{a}{b}", False)
+                else:
+                    w2_q[a, b] = quantise_weight(load_w2(a, b), f"w2_{a}{b}", False)
+
+        out_rows = out.rearrange("(b g t i) j -> b t g i j", b=2, t=PACK, i=8)
+
+        def second_stage(i):
+            c, t = divmod(i, PACK)
+            acc = psum.tile([P, BANK], F32, name="acc")
+            for b in range(2):
+                codes, scales = w2_q[b, c]
+                nc.tensor.matmul_mx(
+                    out=acc[:],
+                    lhsT=codes[:, t * P : (t + 1) * P].bitcast(FP8X4),
+                    lhsT_scale=scales[:, t * P : (t + 1) * P],
+                    rhs=z_q[b][:].bitcast(FP8X4),
+                    rhs_scale=z_sc[b][:],
+                    start=(b == 0),
+                    stop=(b == 1),
+                )
+            nc.scalar.copy(out=ya[i % 4][:, 0:E], in_=acc[:])
+
+        def fetch_back(i, first, width):
+            yr = ring.tile([P, width], F32, name="yr", bufs=3)
+            gate = ring.tile([P, width], F32, name="gate", bufs=2)
+            offsets = pos3_t[:, first // 16 : (first + width) // 16]
+            nc.vector.tensor_copy(out=yr[:], in_=ya[i % 4][:].indirect(offsets))
+            nc.scalar.activation(out=gate[:], in_=yr[:], func=ACT.Sigmoid)
+            return yr, gate
+
+        def apply_gate(i, first, width, gate):
+            mine = h[i][:, first : first + width]
+            nc.vector.scalar_tensor_tensor(
+                out=mine, in0=mine, scalar=gains[:, TILES + i : TILES + i + 1], in1=gate[:], op0=ALU.mult, op1=ALU.mult
+            )
+
+        def finish(i, first, width, yr):
+            mine = h[i][:, first : first + width]
+            nc.vector.tensor_tensor(out=mine, in0=mine, in1=yr[:], op=ALU.add)
+            c, t = divmod(i, PACK)
+            nc.sync.dma_start(out=out_rows[c, t][:, :, first : first + width], in_=mine)
+
+        w2_late = [load_w2(b, 1) for b in range(2)]
+        pieces = [(i, 0, S) for i in range(TILES - 1)] + [(TILES - 1, 0, BANK), (TILES - 1, BANK, BANK)]
+        fetched = {}
+        for n in range(len(pieces) + 2):
+            if n < len(pieces):
+                if pieces[n][1] == 0:
+                    second_stage(pieces[n][0])
+                fetched[n] = fetch_back(*pieces[n])
+            if 1 <= n <= len(pieces):
+                apply_gate(*pieces[n - 1], fetched[n - 1][1])
+            if n >= 2:
+                finish(*pieces[n - 2], fetched[n - 2][0])
+            if n < 2:
+                w2_q[n, 1] = quantise_weight(w2_late[n], f"w2_{n}1", False, z[1])

@@ -47,8 +47,8 @@ def tile_list_sleep_episode_stager_kernel(
         v = [[held([P, BANK], U32, f"v{a}{u}") for u in range(2)] for a in range(PASSES)]
         v_sc = held([P, S], U8, "v_sc")
         v_sc1 = held([P, S], U8, "v_sc1")
-        w4_raw = held([P, PASSES * 2 * H], U8, "w4_raw")
-        w4 = held([P, PASSES * 2 * H], U8, "w4")
+        w4_raw = [held([P, PASSES * 2 * PASS], U8, f"w4_raw{b}") for b in range(2)]
+        w4 = [held([P, PASSES * 2 * PASS], U8, f"w4_{b}") for b in range(2)]
         w4_sc_raw = held([P, PASSES * H], U8, "w4_sc_raw")
         w4_sc = held([P, PASSES * H], U8, "w4_sc")
         gains_rows = held([P, P], F32, "gains_rows")
@@ -57,13 +57,12 @@ def tile_list_sleep_episode_stager_kernel(
         h = [held([P, S], F32, f"h{i}") for i in range(TILES)]
         ya = [held([P, E + S], F32, f"ya{i}") for i in range(4)]
         z = [held([P, E * PACK], BF16, f"z{b}") for b in range(2)]
-        z_q = [held([P, E], U32, f"z_q{b}") for b in range(2)]
         z_sc = [held([P, E], U8, f"z_sc{b}") for b in range(2)]
 
-        nc.vector.memset(table_sc[:].bitcast(I32), 0)
         nc.vector.memset(w4_sc_raw[:].bitcast(I32), 0)
+        nc.vector.memset(table_sc[:].bitcast(I32), 0)
         nc.vector.memset(v_sc1[:].bitcast(I32), 0)
-        nc.vector.memset(gains_rows[:], 0.0)
+        nc.gpsimd.memset(gains_rows[:], 0.0)
         make_identity(nc, ident[:])
 
         def load_table(a):
@@ -72,36 +71,54 @@ def tile_list_sleep_episode_stager_kernel(
             )
 
         def load_w1(a, b):
-            raw = ring.tile([P, PACK, PASS], F32, name="raw", bufs=5)
+            raw = ring.tile([P, PACK, PASS], F32, name="raw", bufs=2)
             rows = w1[a * PASS : (a + 1) * PASS, b * PASS : (b + 1) * PASS]
             nc.sync.dma_start(out=raw[:], in_=rows.rearrange("(p j) c -> p j c", j=PACK))
             return raw
 
+        def load_w4(b):
+            words = w4_words[:, :, 2 * b * PASS : 2 * (b + 1) * PASS].bitcast(I32)
+            nc.sync.dma_start(
+                out=w4_raw[b][:].bitcast(I32).rearrange("p (a c) -> p a c", a=PASSES),
+                in_=words.rearrange("a p c -> p a c"),
+            )
+
+        def deal(dst, src, words):
+            nc.vector.tensor_copy(
+                out=dst[:].bitcast(I32).rearrange("p (s t g w) -> p s t g w", t=PACK, g=16, w=words),
+                in_=src[:].bitcast(I32).rearrange("p (s g t w) -> p s t g w", t=PACK, g=16, w=words),
+            )
+
         def load_w2(b, c):
-            raw = ring.tile([P, PACK, PASS], F32, name="raw", bufs=5)
+            raw = ring.tile([P, PACK, PASS], F32, name="raw", bufs=2)
             rows = w2[b * PASS : (b + 1) * PASS, c * PASS : (c + 1) * PASS]
             rows = rows.rearrange("(g t i) n -> t g i n", t=PACK, i=8)
             for t in range(PACK):
                 nc.sync.dma_start(out=raw[:, t, :], in_=rows[t])
             return raw
 
-        def quantise_weight(raw, name, by_tile, grouped=None):
-            if grouped is None:
-                grouped = ring.tile([P, PASS * PACK], BF16, name="grouped", bufs=3, align_bytes=64)
-            codes = held([P, PASS], U32, name + "_q")
-            scales = held([P, PASS], U8, name + "_sc")
+        def regroup(raw, grouped, t):
             src = raw[:].rearrange("p j (g t u i) -> p t g u j i", t=PACK, u=2, i=4)
             dst = grouped[:].rearrange("p (t g u i j) -> p t g u j i", t=PACK, u=2, i=4, j=PACK)
+            nc.scalar.copy(out=dst[:, t], in_=src[:, t])
+
+        def staging():
+            return ring.tile([P, PASS * PACK], BF16, name="grouped", bufs=3, align_bytes=64)
+
+        def quantise(codes, scales, values):
+            nc.vector.quantize_mx(out=codes.bitcast(FP8X4), scales=scales, in_=values)
+
+        def quantise_weight(raw, name, by_tile, grouped=None):
+            if grouped is None:
+                grouped = staging()
+            codes = held([P, PASS], U32, name + "_q")
+            scales = held([P, PASS], U8, name + "_sc")
             for t in range(PACK):
-                nc.scalar.copy(out=dst[:, t], in_=src[:, t])
-                if by_tile:
-                    nc.vector.quantize_mx(
-                        out=codes[:, t * P : (t + 1) * P].bitcast(FP8X4),
-                        scales=scales[:, t * P : (t + 1) * P],
-                        in_=grouped[:, t * PASS : (t + 1) * PASS],
-                    )
-            if not by_tile:
-                nc.vector.quantize_mx(out=codes[:].bitcast(FP8X4), scales=scales[:], in_=grouped[:])
+                regroup(raw, grouped, t)
+                if by_tile and t == 0:
+                    quantise(codes[:, 0:P], scales[:, 0:P], grouped[:, 0:PASS])
+            done = P if by_tile else 0
+            quantise(codes[:, done:], scales[:, done:], grouped[:, done * PACK :])
             return codes, scales
 
         nc.sync.dma_start(offs_t[:], offs)
@@ -113,37 +130,30 @@ def tile_list_sleep_episode_stager_kernel(
         load_table(0)
         w1_raw = {(0, 0): load_w1(0, 0)}
         load_table(1)
-        nc.sync.dma_start(
-            out=w4_raw[:].bitcast(I32).rearrange("p (a c) -> p a c", a=PASSES),
-            in_=w4_words.bitcast(I32).rearrange("a p c -> p a c"),
-        )
+        w1_raw[1, 0] = load_w1(1, 0)
+        load_w4(0)
         for q in range(4):
             nc.sync.dma_start(
                 out=w4_sc_raw[32 * q : 32 * q + 4, :].bitcast(I32).rearrange("r (a c) -> r a c", a=PASSES),
                 in_=w4_scales[:, 4 * q : 4 * q + 4, :].bitcast(I32).rearrange("a r c -> r a c"),
             )
-        w1_raw[1, 0] = load_w1(1, 0)
         nc.sync.dma_start(pos1_t[:], pos1)
         nc.sync.dma_start(pos2_t[:], pos2)
         for n, vec in enumerate((gp, gs)):
             for b in range(2):
                 row = n * TILES + b * PACK
-                nc.sync.dma_start(
+                nc.gpsimd.dma_start(
                     out=gains_rows[row : row + PACK, :].rearrange("t (g i) -> t g i", i=8),
                     in_=vec[b * PASS : (b + 1) * PASS].rearrange("(g t i) -> t g i", t=PACK, i=8),
                 )
-        w1_raw[0, 1] = load_w1(0, 1)
-        w1_raw[1, 1] = load_w1(1, 1)
         nc.sync.dma_start(pos3_t[:], pos3)
+        load_w4(1)
 
         for q in range(4):
             rows = slice(32 * q, 32 * q + 8)
             nc.vector.tensor_copy(out=table_sc[rows, :].bitcast(I32), in_=table_sc_rows[rows, :].bitcast(I32))
         nc.vector.tensor_copy(out=v_sc[:], in_=table_sc[:].indirect(offs_t[:]))
-        for q in range(4):
-            nc.scalar.dma_start(
-                out=v_sc1[32 * q : 32 * q + 4, :].bitcast(I32), in_=v_sc[32 * q + 4 : 32 * q + 8, :].bitcast(I32)
-            )
+        nc.gpsimd.dma_start(out=v_sc1[0:100, :].bitcast(I32), in_=v_sc[4:104, :].bitcast(I32))
 
         def gather_table(a):
             for u in range(2):
@@ -153,12 +163,9 @@ def tile_list_sleep_episode_stager_kernel(
         gather_table(0)
         w1_q[0, 0] = quantise_weight(w1_raw[0, 0], "w1_00", True)
         gather_table(1)
-        for dst, src, words in ((w4, w4_raw, 4), (w4_sc, w4_sc_raw, 2)):
-            nc.vector.tensor_copy(
-                out=dst[:].bitcast(I32).rearrange("p (s t g w) -> p s t g w", t=PACK, g=16, w=words),
-                in_=src[:].bitcast(I32).rearrange("p (s g t w) -> p s t g w", t=PACK, g=16, w=words),
-            )
         w1_q[1, 0] = quantise_weight(w1_raw[1, 0], "w1_10", True)
+        deal(w4_sc, w4_sc_raw, 2)
+        deal(w4[0], w4_raw[0], 4)
 
         def turn_gains():
             turned = psum.tile([P, BANK], F32, name="acc")
@@ -183,9 +190,10 @@ def tile_list_sleep_episode_stager_kernel(
             acc_b = psum.tile([P, BANK], F32, name="acc")
             for a in range(PASSES):
                 first = a * H + i * P
+                word = a * PASS + t * P
                 nc.tensor.matmul_mx(
                     out=acc_b[:],
-                    lhsT=w4[:, 2 * first : 2 * (first + P)].bitcast(FP4X4),
+                    lhsT=w4[b][:, 2 * word : 2 * (word + P)].bitcast(FP4X4),
                     lhsT_scale=w4_sc[:, first : first + P],
                     rhs=v[a][u][:].bitcast(FP8X4),
                     rhs_scale=(v_sc, v_sc1)[a][:, cols],
@@ -196,45 +204,67 @@ def tile_list_sleep_episode_stager_kernel(
             nc.scalar.copy(out=a_sb, in_=acc_a[:])
             nc.vector.tensor_tensor(out=h[i][:, cols], in0=acc_b[:], in1=a_sb, op=ALU.max)
 
-        def pick_first(i):
-            picked = ring.tile([P, E], F32, name="picked")
-            nc.vector.tensor_copy(out=picked[:], in_=h[i][:].indirect(pos1_t[:]))
-            return picked
+        last_picked = keep.tile([P, E], F32, name="last_picked", tag="turn", align_bytes=64)
 
-        def join_pair(i, picked):
+        def picked(i):
+            return last_picked[:] if i == TILES - 1 else ya[(i + 1) % 4][:, E + BANK :]
+
+        def pick_first(i):
+            nc.vector.tensor_copy(out=picked(i), in_=h[i][:].indirect(pos1_t[:]))
+
+        def join_pair(i):
+            pair = ya[(i + 2) % 4][:, E : E + BANK]
+            if i == TILES - 1:
+                nc.vector.tensor_tensor(out=pair, in0=h[i][:].indirect(pos2_t[:]), in1=picked(i), op=ALU.add)
+            else:
+                nc.vector.tensor_copy(out=pair, in_=h[i][:].indirect(pos2_t[:]))
+                nc.gpsimd.tensor_tensor(out=pair, in0=pair, in1=picked(i), op=ALU.add)
+
+        def scale_pair(i):
             b, t = divmod(i, PACK)
-            pair = ring.tile([P, E], F32, name="pair", bufs=3)
-            nc.vector.tensor_tensor(out=pair[:], in0=h[i][:].indirect(pos2_t[:]), in1=picked[:], op=ALU.add)
             nc.scalar.activation(
                 out=z[b][:].rearrange("p (m t) -> p t m", t=PACK)[:, t, :],
-                in_=pair[:],
+                in_=ya[(i + 2) % 4][:, E : E + BANK],
                 func=ACT.Copy,
                 scale=gains[:, i : i + 1],
             )
-            if t == PACK - 1:
-                nc.vector.quantize_mx(out=z_q[b][:].bitcast(FP8X4), scales=z_sc[b][:], in_=z[b][:])
 
         w2_q = {}
+        w2_grouped = []
         later = [
             ("w1", 0, 1), ("w1", 1, 1), ("w2", 0, 0), ("w2", 1, 0),
         ]
-        for i in range(TILES + 1):
+        for i in range(TILES + 2):
             if i < TILES:
                 first_stage(i, 0)
-            if i > 0:
-                picked = pick_first(i - 1)
+            if i >= 2:
+                join_pair(i - 2)
             if i < TILES:
                 first_stage(i, 1)
             if i == 0:
                 turn_gains()
-            if i > 0:
-                join_pair(i - 1, picked)
+                deal(w4[1], w4_raw[1], 4)
+            if i >= 2:
+                scale_pair(i - 2)
+            if 1 <= i <= TILES:
+                pick_first(i - 1)
             if i < len(later):
                 kind, a, b = later[i]
                 if kind == "w1":
-                    w1_q[a, b] = quantise_weight(w1_raw[a, b], f"w1_{a}{b}", False)
+                    w1_q[a, b] = quantise_weight(load_w1(a, b), f"w1_{a}{b}", False)
                 else:
-                    w2_q[a, b] = quantise_weight(load_w2(a, b), f"w2_{a}{b}", False)
+                    raw = load_w2(a, b)
+                    w2_grouped.append(staging())
+                    for t in range(PACK):
+                        regroup(raw, w2_grouped[a], t)
+
+        turn_codes = keep.tile([P, 3 * PASS], U32, name="turn_codes", tag="turn", align_bytes=64)
+        z_q = [turn_codes[:, 0:E], held([P, E], U32, "z_q1")[:]]
+        quantise(z_q[0], z_sc[0][:], z[0][:])
+        for b in range(2):
+            w2_q[b, 0] = turn_codes[:, (b + 1) * PASS : (b + 2) * PASS], held([P, PASS], U8, f"w2_{b}0_sc")
+            quantise(w2_q[b, 0][0], w2_q[b, 0][1][:], w2_grouped[b][:])
+        quantise(z_q[1], z_sc[1][:], z[1][:])
 
         out_rows = out.rearrange("(b g t i) j -> b t g i j", b=2, t=PACK, i=8)
 
@@ -247,7 +277,7 @@ def tile_list_sleep_episode_stager_kernel(
                     out=acc[:],
                     lhsT=codes[:, t * P : (t + 1) * P].bitcast(FP8X4),
                     lhsT_scale=scales[:, t * P : (t + 1) * P],
-                    rhs=z_q[b][:].bitcast(FP8X4),
+                    rhs=z_q[b].bitcast(FP8X4),
                     rhs_scale=z_sc[b][:],
                     start=(b == 0),
                     stop=(b == 1),
@@ -263,14 +293,16 @@ def tile_list_sleep_episode_stager_kernel(
             return yr, gate
 
         def apply_gate(i, first, width, gate):
+            gated = ring.tile([P, width], F32, name="gated", bufs=1)
+            engine = nc.vector if i == TILES - 1 else nc.gpsimd
+            engine.tensor_tensor(out=gated[:], in0=h[i][:, first : first + width], in1=gate[:], op=ALU.mult)
+            return gated
+
+        def finish(i, first, width, yr, gated):
             mine = h[i][:, first : first + width]
             nc.vector.scalar_tensor_tensor(
-                out=mine, in0=mine, scalar=gains[:, TILES + i : TILES + i + 1], in1=gate[:], op0=ALU.mult, op1=ALU.mult
+                out=mine, in0=gated[:], scalar=gains[:, TILES + i : TILES + i + 1], in1=yr[:], op0=ALU.mult, op1=ALU.add
             )
-
-        def finish(i, first, width, yr):
-            mine = h[i][:, first : first + width]
-            nc.vector.tensor_tensor(out=mine, in0=mine, in1=yr[:], op=ALU.add)
             c, t = divmod(i, PACK)
             nc.sync.dma_start(out=out_rows[c, t][:, :, first : first + width], in_=mine)
 
@@ -282,9 +314,9 @@ def tile_list_sleep_episode_stager_kernel(
                 if pieces[n][1] == 0:
                     second_stage(pieces[n][0])
                 fetched[n] = fetch_back(*pieces[n])
-            if 1 <= n <= len(pieces):
-                apply_gate(*pieces[n - 1], fetched[n - 1][1])
             if n >= 2:
-                finish(*pieces[n - 2], fetched[n - 2][0])
+                finish(*pieces[n - 2], fetched[n - 2][0], gated)
+            if 1 <= n <= len(pieces):
+                gated = apply_gate(*pieces[n - 1], fetched[n - 1][1])
             if n < 2:
                 w2_q[n, 1] = quantise_weight(w2_late[n], f"w2_{n}1", False, z[1])

@@ -103,14 +103,13 @@ def tile_list_sleep_episode_stager_kernel(
             nc.scalar.copy(out=dst[:, t], in_=src[:, t])
 
         def staging():
-            return ring.tile([P, PASS * PACK], BF16, name="grouped", bufs=3, align_bytes=64)
+            return ring.tile([P, PASS * PACK], BF16, name="grouped", bufs=4, align_bytes=64)
 
         def quantise(codes, scales, values):
             nc.vector.quantize_mx(out=codes.bitcast(FP8X4), scales=scales, in_=values)
 
-        def quantise_weight(raw, name, by_tile, grouped=None):
-            if grouped is None:
-                grouped = staging()
+        def quantise_weight(raw, name, by_tile):
+            grouped = staging()
             codes = held([P, PASS], U32, name + "_q")
             scales = held([P, PASS], U8, name + "_sc")
             for t in range(PACK):
@@ -142,7 +141,7 @@ def tile_list_sleep_episode_stager_kernel(
         for n, vec in enumerate((gp, gs)):
             for b in range(2):
                 row = n * TILES + b * PACK
-                nc.gpsimd.dma_start(
+                nc.sync.dma_start(
                     out=gains_rows[row : row + PACK, :].rearrange("t (g i) -> t g i", i=8),
                     in_=vec[b * PASS : (b + 1) * PASS].rearrange("(g t i) -> t g i", t=PACK, i=8),
                 )
@@ -222,17 +221,19 @@ def tile_list_sleep_episode_stager_kernel(
 
         def scale_pair(i):
             b, t = divmod(i, PACK)
-            nc.scalar.activation(
-                out=z[b][:].rearrange("p (m t) -> p t m", t=PACK)[:, t, :],
-                in_=ya[(i + 2) % 4][:, E : E + BANK],
-                func=ACT.Copy,
-                scale=gains[:, i : i + 1],
-            )
+            slot = z[b][:].rearrange("p (m t) -> p t m", t=PACK)[:, t, :]
+            pair = ya[(i + 2) % 4][:, E : E + BANK]
+            if i < TILES - 2:
+                nc.gpsimd.tensor_scalar(
+                    out=slot, in0=pair, scalar1=gains[:, i : i + 1], scalar2=0.0, op0=ALU.mult, op1=ALU.add
+                )
+            else:
+                nc.scalar.activation(out=slot, in_=pair, func=ACT.Copy, scale=gains[:, i : i + 1])
 
         w2_q = {}
-        w2_grouped = []
+        w2_grouped = {}
         later = [
-            ("w1", 0, 1), ("w1", 1, 1), ("w2", 0, 0), ("w2", 1, 0),
+            ("w1", 0, 1), ("w1", 1, 1), ("w2", 0, 0), ("w2", 1, 0), ("w2", 0, 1), ("w2", 1, 1),
         ]
         for i in range(TILES + 2):
             if i < TILES:
@@ -254,17 +255,23 @@ def tile_list_sleep_episode_stager_kernel(
                     w1_q[a, b] = quantise_weight(load_w1(a, b), f"w1_{a}{b}", False)
                 else:
                     raw = load_w2(a, b)
-                    w2_grouped.append(staging())
+                    w2_grouped[a, b] = staging()
                     for t in range(PACK):
-                        regroup(raw, w2_grouped[a], t)
+                        regroup(raw, w2_grouped[a, b], t)
 
-        turn_codes = keep.tile([P, 3 * PASS], U32, name="turn_codes", tag="turn", align_bytes=64)
+        turn_codes = keep.tile([P, 5 * PASS], U32, name="turn_codes", tag="turn", align_bytes=64)
+
+        def quantise_w2(c):
+            for b in range(2):
+                first = (1 + 2 * c + b) * PASS
+                w2_q[b, c] = turn_codes[:, first : first + PASS], held([P, PASS], U8, f"w2_{b}{c}_sc")
+                quantise(w2_q[b, c][0], w2_q[b, c][1][:], w2_grouped[b, c][:])
+
         z_q = [turn_codes[:, 0:E], held([P, E], U32, "z_q1")[:]]
         quantise(z_q[0], z_sc[0][:], z[0][:])
-        for b in range(2):
-            w2_q[b, 0] = turn_codes[:, (b + 1) * PASS : (b + 2) * PASS], held([P, PASS], U8, f"w2_{b}0_sc")
-            quantise(w2_q[b, 0][0], w2_q[b, 0][1][:], w2_grouped[b][:])
+        quantise_w2(0)
         quantise(z_q[1], z_sc[1][:], z[1][:])
+        quantise_w2(1)
 
         out_rows = out.rearrange("(b g t i) j -> b t g i j", b=2, t=PACK, i=8)
 
@@ -284,39 +291,44 @@ def tile_list_sleep_episode_stager_kernel(
                 )
             nc.scalar.copy(out=ya[i % 4][:, 0:E], in_=acc[:])
 
-        def fetch_back(i, first, width):
-            yr = ring.tile([P, width], F32, name="yr", bufs=3)
-            gate = ring.tile([P, width], F32, name="gate", bufs=2)
-            offsets = pos3_t[:, first // 16 : (first + width) // 16]
-            nc.vector.tensor_copy(out=yr[:], in_=ya[i % 4][:].indirect(offsets))
-            nc.scalar.activation(out=gate[:], in_=yr[:], func=ACT.Sigmoid)
-            return yr, gate
+        def fetch_back(i):
+            yr = ring.tile([P, S], F32, name="yr", bufs=3)
+            nc.vector.tensor_copy(out=yr[:], in_=ya[i % 4][:].indirect(pos3_t[:]))
+            return yr
 
-        def apply_gate(i, first, width, gate):
-            gated = ring.tile([P, width], F32, name="gated", bufs=1)
+        def pieces(i):
+            width = BANK if i == TILES - 1 else S
+            return [slice(first, first + width) for first in range(0, S, width)]
+
+        def apply_gate(i, yr):
+            gate = ring.tile([P, S], F32, name="gate", bufs=2)
+            gated = ring.tile([P, S], F32, name="gated", bufs=2)
             engine = nc.vector if i == TILES - 1 else nc.gpsimd
-            engine.tensor_tensor(out=gated[:], in0=h[i][:, first : first + width], in1=gate[:], op=ALU.mult)
+            for cols in pieces(i):
+                nc.scalar.activation(out=gate[:, cols], in_=yr[:, cols], func=ACT.Sigmoid)
+            for cols in pieces(i):
+                engine.tensor_tensor(out=gated[:, cols], in0=h[i][:, cols], in1=gate[:, cols], op=ALU.mult)
             return gated
 
-        def finish(i, first, width, yr, gated):
-            mine = h[i][:, first : first + width]
-            nc.vector.scalar_tensor_tensor(
-                out=mine, in0=gated[:], scalar=gains[:, TILES + i : TILES + i + 1], in1=yr[:], op0=ALU.mult, op1=ALU.add
-            )
+        def finish(i, yr, gated):
             c, t = divmod(i, PACK)
-            nc.sync.dma_start(out=out_rows[c, t][:, :, first : first + width], in_=mine)
+            for cols in pieces(i):
+                nc.vector.scalar_tensor_tensor(
+                    out=h[i][:, cols],
+                    in0=gated[:, cols],
+                    scalar=gains[:, TILES + i : TILES + i + 1],
+                    in1=yr[:, cols],
+                    op0=ALU.mult,
+                    op1=ALU.add,
+                )
+                nc.sync.dma_start(out=out_rows[c, t][:, :, cols], in_=h[i][:, cols])
 
-        w2_late = [load_w2(b, 1) for b in range(2)]
-        pieces = [(i, 0, S) for i in range(TILES - 1)] + [(TILES - 1, 0, BANK), (TILES - 1, BANK, BANK)]
-        fetched = {}
-        for n in range(len(pieces) + 2):
-            if n < len(pieces):
-                if pieces[n][1] == 0:
-                    second_stage(pieces[n][0])
-                fetched[n] = fetch_back(*pieces[n])
+        fetched, gated = {}, {}
+        for n in range(TILES + 2):
+            if n < TILES:
+                second_stage(n)
+                fetched[n] = fetch_back(n)
             if n >= 2:
-                finish(*pieces[n - 2], fetched[n - 2][0], gated)
-            if 1 <= n <= len(pieces):
-                gated = apply_gate(*pieces[n - 1], fetched[n - 1][1])
-            if n < 2:
-                w2_q[n, 1] = quantise_weight(w2_late[n], f"w2_{n}1", False, z[1])
+                finish(n - 2, fetched[n - 2], gated[n - 2])
+            if n < TILES:
+                gated[n] = apply_gate(n, fetched[n])

@@ -83,8 +83,8 @@ def tile_list_sleep_episode_stager_kernel(
                 in_=words.rearrange("a p c -> p a c"),
             )
 
-        def deal(dst, src, words):
-            nc.vector.tensor_copy(
+        def deal(dst, src, words, engine=nc.vector):
+            engine.tensor_copy(
                 out=dst[:].bitcast(I32).rearrange("p (s t g w) -> p s t g w", t=PACK, g=16, w=words),
                 in_=src[:].bitcast(I32).rearrange("p (s g t w) -> p s t g w", t=PACK, g=16, w=words),
             )
@@ -165,6 +165,7 @@ def tile_list_sleep_episode_stager_kernel(
         w1_q[1, 0] = quantise_weight(w1_raw[1, 0], "w1_10", True)
         deal(w4_sc, w4_sc_raw, 2)
         deal(w4[0], w4_raw[0], 4)
+        deal(w4[1], w4_raw[1], 4, nc.gpsimd)
 
         def turn_gains():
             turned = psum.tile([P, BANK], F32, name="acc")
@@ -213,7 +214,7 @@ def tile_list_sleep_episode_stager_kernel(
 
         def join_pair(i):
             pair = ya[(i + 2) % 4][:, E : E + BANK]
-            if i == TILES - 1:
+            if i >= PACK:
                 nc.vector.tensor_tensor(out=pair, in0=h[i][:].indirect(pos2_t[:]), in1=picked(i), op=ALU.add)
             else:
                 nc.vector.tensor_copy(out=pair, in_=h[i][:].indirect(pos2_t[:]))
@@ -242,15 +243,14 @@ def tile_list_sleep_episode_stager_kernel(
                 join_pair(i - 2)
             if i < TILES:
                 first_stage(i, 1)
-            if i == 0:
+            if i == 1:
                 turn_gains()
-                deal(w4[1], w4_raw[1], 4)
             if i >= 2:
                 scale_pair(i - 2)
             if 1 <= i <= TILES:
                 pick_first(i - 1)
-            if i < len(later):
-                kind, a, b = later[i]
+            if 2 <= i < len(later) + 2:
+                kind, a, b = later[i - 2]
                 if kind == "w1":
                     w1_q[a, b] = quantise_weight(load_w1(a, b), f"w1_{a}{b}", False)
                 else:
@@ -292,7 +292,7 @@ def tile_list_sleep_episode_stager_kernel(
             nc.scalar.copy(out=ya[i % 4][:, 0:E], in_=acc[:])
 
         def fetch_back(i):
-            yr = ring.tile([P, S], F32, name="yr", bufs=3)
+            yr = ring.tile([P, S], F32, name="yr", bufs=4)
             nc.vector.tensor_copy(out=yr[:], in_=ya[i % 4][:].indirect(pos3_t[:]))
             return yr
 
@@ -301,9 +301,9 @@ def tile_list_sleep_episode_stager_kernel(
             return [slice(first, first + width) for first in range(0, S, width)]
 
         def apply_gate(i, yr):
-            gate = ring.tile([P, S], F32, name="gate", bufs=2)
-            gated = ring.tile([P, S], F32, name="gated", bufs=2)
-            engine = nc.vector if i == TILES - 1 else nc.gpsimd
+            gate = ring.tile([P, S], F32, name="gate", bufs=3)
+            gated = ring.tile([P, S], F32, name="gated", bufs=3)
+            engine = nc.vector if i >= TILES - 2 else nc.gpsimd
             for cols in pieces(i):
                 nc.scalar.activation(out=gate[:, cols], in_=yr[:, cols], func=ACT.Sigmoid)
             for cols in pieces(i):
@@ -324,11 +324,14 @@ def tile_list_sleep_episode_stager_kernel(
                 nc.sync.dma_start(out=out_rows[c, t][:, :, cols], in_=h[i][:, cols])
 
         fetched, gated = {}, {}
-        for n in range(TILES + 2):
+        for n in range(4):
+            second_stage(n)
+        for n in range(TILES + 3):
             if n < TILES:
-                second_stage(n)
                 fetched[n] = fetch_back(n)
-            if n >= 2:
-                finish(n - 2, fetched[n - 2], gated[n - 2])
+            if n + 4 < TILES:
+                second_stage(n + 4)
+            if n >= 3:
+                finish(n - 3, fetched[n - 3], gated[n - 3])
             if n < TILES:
                 gated[n] = apply_gate(n, fetched[n])

@@ -23,6 +23,21 @@ PASS = P * PACK
 BANK = 512
 PASSES = K // PASS
 TILES = H // P
+HALVES = S // BANK
+BLOCKS = P // 8
+RUN = 8
+QUADRANTS = 4
+
+WINDOWS = 4
+RAW_BUFS = 2
+STAGING_BUFS = 4
+FETCH_BUFS = 4
+GATE_BUFS = 3
+UNSKEWED = 2
+CAST_LAG = 2
+GPSIMD_ADDS = 4
+GPSIMD_SCALES = 6
+GPSIMD_GATES = 6
 
 
 def tile_list_sleep_episode_stager_kernel(
@@ -44,20 +59,20 @@ def tile_list_sleep_episode_stager_kernel(
         table = [held([P, T], U32, f"table{a}") for a in range(PASSES)]
         table_sc = held([P, T], U8, "table_sc")
         table_sc_rows = held([P, T], U8, "table_sc_rows")
-        v = [[held([P, BANK], U32, f"v{a}{u}") for u in range(2)] for a in range(PASSES)]
+        v = [[held([P, BANK], U32, f"v{a}{u}") for u in range(HALVES)] for a in range(PASSES)]
         v_sc = held([P, S], U8, "v_sc")
         v_sc1 = held([P, S], U8, "v_sc1")
-        w4_raw = [held([P, PASSES * 2 * PASS], U8, f"w4_raw{b}") for b in range(2)]
-        w4 = [held([P, PASSES * 2 * PASS], U8, f"w4_{b}") for b in range(2)]
+        w4_raw = [held([P, PASSES * 2 * PASS], U8, f"w4_raw{b}") for b in range(PASSES)]
+        w4 = [held([P, PASSES * 2 * PASS], U8, f"w4_{b}") for b in range(PASSES)]
         w4_sc_raw = held([P, PASSES * H], U8, "w4_sc_raw")
         w4_sc = held([P, PASSES * H], U8, "w4_sc")
         gains_rows = held([P, P], F32, "gains_rows")
         ident = held([P, P], F32, "ident")
         gains = held([P, 2 * TILES], F32, "gains")
         h = [held([P, S], F32, f"h{i}") for i in range(TILES)]
-        ya = [held([P, E + S], F32, f"ya{i}") for i in range(4)]
-        z = [held([P, E * PACK], BF16, f"z{b}") for b in range(2)]
-        z_sc = [held([P, E], U8, f"z_sc{b}") for b in range(2)]
+        ya = [held([P, E + S], F32, f"ya{i}") for i in range(WINDOWS)]
+        z = [held([P, E * PACK], BF16, f"z{b}") for b in range(PASSES)]
+        z_sc = [held([P, E], U8, f"z_sc{b}") for b in range(PASSES)]
 
         nc.vector.memset(w4_sc_raw[:].bitcast(I32), 0)
         nc.vector.memset(table_sc[:].bitcast(I32), 0)
@@ -71,7 +86,7 @@ def tile_list_sleep_episode_stager_kernel(
             )
 
         def load_w1(a, b):
-            raw = ring.tile([P, PACK, PASS], F32, name="raw", bufs=2)
+            raw = ring.tile([P, PACK, PASS], F32, name="raw", bufs=RAW_BUFS)
             rows = w1[a * PASS : (a + 1) * PASS, b * PASS : (b + 1) * PASS]
             nc.sync.dma_start(out=raw[:], in_=rows.rearrange("(p j) c -> p j c", j=PACK))
             return raw
@@ -83,89 +98,90 @@ def tile_list_sleep_episode_stager_kernel(
                 in_=words.rearrange("a p c -> p a c"),
             )
 
-        def deal(dst, src, words, engine=nc.vector):
+        def deal(dst, src, words, engine):
             engine.tensor_copy(
-                out=dst[:].bitcast(I32).rearrange("p (s t g w) -> p s t g w", t=PACK, g=16, w=words),
-                in_=src[:].bitcast(I32).rearrange("p (s g t w) -> p s t g w", t=PACK, g=16, w=words),
+                out=dst[:].bitcast(I32).rearrange("p (s t g w) -> p s t g w", t=PACK, g=BLOCKS, w=words),
+                in_=src[:].bitcast(I32).rearrange("p (s g t w) -> p s t g w", t=PACK, g=BLOCKS, w=words),
             )
 
         def load_w2(b, c):
-            raw = ring.tile([P, PACK, PASS], F32, name="raw", bufs=2)
+            raw = ring.tile([P, PACK, PASS], F32, name="raw", bufs=RAW_BUFS)
             rows = w2[b * PASS : (b + 1) * PASS, c * PASS : (c + 1) * PASS]
-            rows = rows.rearrange("(g t i) n -> t g i n", t=PACK, i=8)
+            rows = rows.rearrange("(g t e) n -> t g e n", t=PACK, e=RUN)
             for t in range(PACK):
                 nc.sync.dma_start(out=raw[:, t, :], in_=rows[t])
             return raw
 
         def regroup(raw, grouped, t):
-            src = raw[:].rearrange("p j (g t u i) -> p t g u j i", t=PACK, u=2, i=4)
-            dst = grouped[:].rearrange("p (t g u i j) -> p t g u j i", t=PACK, u=2, i=4, j=PACK)
+            src = raw[:].rearrange("p j (g t u n) -> p t g u j n", t=PACK, u=2, n=4)
+            dst = grouped[:].rearrange("p (t g u n j) -> p t g u j n", t=PACK, u=2, n=4, j=PACK)
             nc.scalar.copy(out=dst[:, t], in_=src[:, t])
 
         def staging():
-            return ring.tile([P, PASS * PACK], BF16, name="grouped", bufs=4, align_bytes=64)
+            return ring.tile([P, PASS * PACK], BF16, name="grouped", bufs=STAGING_BUFS, align_bytes=64)
 
         def quantise(codes, scales, values):
             nc.vector.quantize_mx(out=codes.bitcast(FP8X4), scales=scales, in_=values)
 
-        def quantise_weight(raw, name, by_tile):
+        def quantise_w1(raw, a, b):
             grouped = staging()
-            codes = held([P, PASS], U32, name + "_q")
-            scales = held([P, PASS], U8, name + "_sc")
+            codes = held([P, PASS], U32, f"w1_{a}{b}_q")
+            scales = held([P, PASS], U8, f"w1_{a}{b}_sc")
             for t in range(PACK):
                 regroup(raw, grouped, t)
-                if by_tile and t == 0:
+                if b == 0 and t == 0:
                     quantise(codes[:, 0:P], scales[:, 0:P], grouped[:, 0:PASS])
-            done = P if by_tile else 0
+            done = P if b == 0 else 0
             quantise(codes[:, done:], scales[:, done:], grouped[:, done * PACK :])
             return codes, scales
 
         nc.sync.dma_start(offs_t[:], offs)
-        for q in range(4):
+        for q in range(QUADRANTS):
             nc.sync.dma_start(
                 out=table_sc_rows[32 * q : 32 * q + 8, :].bitcast(I32),
                 in_=tab_scales[:, 4 * q : 4 * q + 4, :].bitcast(I32),
             )
         load_table(0)
-        w1_raw = {(0, 0): load_w1(0, 0)}
+        w1_first = load_w1(0, 0)
         load_table(1)
-        w1_raw[1, 0] = load_w1(1, 0)
         load_w4(0)
-        for q in range(4):
+        for q in range(QUADRANTS):
             nc.sync.dma_start(
                 out=w4_sc_raw[32 * q : 32 * q + 4, :].bitcast(I32).rearrange("r (a c) -> r a c", a=PASSES),
                 in_=w4_scales[:, 4 * q : 4 * q + 4, :].bitcast(I32).rearrange("a r c -> r a c"),
             )
+        w1_second = load_w1(1, 0)
         nc.sync.dma_start(pos1_t[:], pos1)
         nc.sync.dma_start(pos2_t[:], pos2)
         for n, vec in enumerate((gp, gs)):
-            for b in range(2):
+            for b in range(PASSES):
                 row = n * TILES + b * PACK
                 nc.sync.dma_start(
-                    out=gains_rows[row : row + PACK, :].rearrange("t (g i) -> t g i", i=8),
-                    in_=vec[b * PASS : (b + 1) * PASS].rearrange("(g t i) -> t g i", t=PACK, i=8),
+                    out=gains_rows[row : row + PACK, :].rearrange("t (g e) -> t g e", e=RUN),
+                    in_=vec[b * PASS : (b + 1) * PASS].rearrange("(g t e) -> t g e", t=PACK, e=RUN),
                 )
         nc.sync.dma_start(pos3_t[:], pos3)
         load_w4(1)
 
-        for q in range(4):
+        for q in range(QUADRANTS):
             rows = slice(32 * q, 32 * q + 8)
             nc.vector.tensor_copy(out=table_sc[rows, :].bitcast(I32), in_=table_sc_rows[rows, :].bitcast(I32))
         nc.vector.tensor_copy(out=v_sc[:], in_=table_sc[:].indirect(offs_t[:]))
         nc.gpsimd.dma_start(out=v_sc1[0:100, :].bitcast(I32), in_=v_sc[4:104, :].bitcast(I32))
 
         def gather_table(a):
-            for u in range(2):
-                nc.vector.tensor_copy(out=v[a][u][:], in_=table[a][:].indirect(offs_t[:, 32 * u : 32 * (u + 1)]))
+            for u in range(HALVES):
+                offsets = offs_t[:, u * BANK // 16 : (u + 1) * BANK // 16]
+                nc.vector.tensor_copy(out=v[a][u][:], in_=table[a][:].indirect(offsets))
 
         w1_q = {}
         gather_table(0)
-        w1_q[0, 0] = quantise_weight(w1_raw[0, 0], "w1_00", True)
+        w1_q[0, 0] = quantise_w1(w1_first, 0, 0)
         gather_table(1)
-        w1_q[1, 0] = quantise_weight(w1_raw[1, 0], "w1_10", True)
-        deal(w4_sc, w4_sc_raw, 2)
-        deal(w4[0], w4_raw[0], 4)
-        deal(w4[1], w4_raw[1], 4, nc.gpsimd)
+        deal(w4_sc, w4_sc_raw, RUN // 4, nc.vector)
+        deal(w4[0], w4_raw[0], 2 * RUN // 4, nc.vector)
+        w1_q[1, 0] = quantise_w1(w1_second, 1, 0)
+        deal(w4[1], w4_raw[1], 2 * RUN // 4, nc.gpsimd)
 
         def turn_gains():
             turned = psum.tile([P, BANK], F32, name="acc")
@@ -189,32 +205,38 @@ def tile_list_sleep_episode_stager_kernel(
                 )
             acc_b = psum.tile([P, BANK], F32, name="acc")
             for a in range(PASSES):
-                first = a * H + i * P
-                word = a * PASS + t * P
+                scale_col = a * H + i * P
+                word_col = a * PASS + t * P
                 nc.tensor.matmul_mx(
                     out=acc_b[:],
-                    lhsT=w4[b][:, 2 * word : 2 * (word + P)].bitcast(FP4X4),
-                    lhsT_scale=w4_sc[:, first : first + P],
+                    lhsT=w4[b][:, 2 * word_col : 2 * (word_col + P)].bitcast(FP4X4),
+                    lhsT_scale=w4_sc[:, scale_col : scale_col + P],
                     rhs=v[a][u][:].bitcast(FP8X4),
                     rhs_scale=(v_sc, v_sc1)[a][:, cols],
                     start=(a == 0),
                     stop=(a == PASSES - 1),
                 )
-            a_sb = ya[i % 4][:, E + u * BANK : E + (u + 1) * BANK]
+            a_sb = ya[i % WINDOWS][:, E + u * BANK : E + (u + 1) * BANK]
             nc.scalar.copy(out=a_sb, in_=acc_a[:])
             nc.vector.tensor_tensor(out=h[i][:, cols], in0=acc_b[:], in1=a_sb, op=ALU.max)
 
         last_picked = keep.tile([P, E], F32, name="last_picked", tag="turn", align_bytes=64)
+        early = [ring.tile([P, E], F32, name="yr", bufs=FETCH_BUFS) for n in range(2 * UNSKEWED)]
 
         def picked(i):
-            return last_picked[:] if i == TILES - 1 else ya[(i + 1) % 4][:, E + BANK :]
+            if i < UNSKEWED:
+                return early[2 * i][:]
+            return last_picked[:] if i == TILES - 1 else ya[(i + 1) % WINDOWS][:, E + BANK :]
+
+        def paired(i):
+            return early[2 * i + 1][:] if i < UNSKEWED else ya[(i + 2) % WINDOWS][:, E : E + BANK]
 
         def pick_first(i):
             nc.vector.tensor_copy(out=picked(i), in_=h[i][:].indirect(pos1_t[:]))
 
         def join_pair(i):
-            pair = ya[(i + 2) % 4][:, E : E + BANK]
-            if i >= PACK:
+            pair = paired(i)
+            if i >= GPSIMD_ADDS:
                 nc.vector.tensor_tensor(out=pair, in0=h[i][:].indirect(pos2_t[:]), in1=picked(i), op=ALU.add)
             else:
                 nc.vector.tensor_copy(out=pair, in_=h[i][:].indirect(pos2_t[:]))
@@ -222,48 +244,57 @@ def tile_list_sleep_episode_stager_kernel(
 
         def scale_pair(i):
             b, t = divmod(i, PACK)
-            slot = z[b][:].rearrange("p (m t) -> p t m", t=PACK)[:, t, :]
-            pair = ya[(i + 2) % 4][:, E : E + BANK]
-            if i < TILES - 2:
+            place = z[b][:].rearrange("p (m t) -> p t m", t=PACK)[:, t, :]
+            pair = paired(i)
+            if i < GPSIMD_SCALES:
                 nc.gpsimd.tensor_scalar(
-                    out=slot, in0=pair, scalar1=gains[:, i : i + 1], scalar2=0.0, op0=ALU.mult, op1=ALU.add
+                    out=place, in0=pair, scalar1=gains[:, i : i + 1], scalar2=0.0, op0=ALU.mult, op1=ALU.add
                 )
             else:
-                nc.scalar.activation(out=slot, in_=pair, func=ACT.Copy, scale=gains[:, i : i + 1])
+                nc.scalar.activation(out=place, in_=pair, func=ACT.Copy, scale=gains[:, i : i + 1])
 
-        w2_q = {}
         w2_grouped = {}
-        later = [
-            ("w1", 0, 1), ("w1", 1, 1), ("w2", 0, 0), ("w2", 1, 0), ("w2", 0, 1), ("w2", 1, 1),
-        ]
+
+        def prepare_w1(a):
+            w1_q[a, 1] = quantise_w1(load_w1(a, 1), a, 1)
+
+        def prepare_w2(b, c):
+            raw = load_w2(b, c)
+            w2_grouped[b, c] = staging()
+            for t in range(PACK):
+                regroup(raw, w2_grouped[b, c], t)
+
         for i in range(TILES + 2):
             if i < TILES:
                 first_stage(i, 0)
-            if i >= 2:
+            if i - 2 >= UNSKEWED:
                 join_pair(i - 2)
             if i < TILES:
                 first_stage(i, 1)
-            if i == 1:
+            if i == UNSKEWED - 1:
                 turn_gains()
-            if i >= 2:
+                scale_pair(i - 1)
+            if i - 2 >= UNSKEWED:
                 scale_pair(i - 2)
-            if 1 <= i <= TILES:
+            if i < UNSKEWED:
+                pick_first(i)
+                join_pair(i)
+            if i == UNSKEWED - 1:
+                scale_pair(i)
+            if UNSKEWED <= i - 1 < TILES:
                 pick_first(i - 1)
-            if 2 <= i < len(later) + 2:
-                kind, a, b = later[i - 2]
-                if kind == "w1":
-                    w1_q[a, b] = quantise_weight(load_w1(a, b), f"w1_{a}{b}", False)
-                else:
-                    raw = load_w2(a, b)
-                    w2_grouped[a, b] = staging()
-                    for t in range(PACK):
-                        regroup(raw, w2_grouped[a, b], t)
+            chunk = i - CAST_LAG
+            if 0 <= chunk < PASSES:
+                prepare_w1(chunk)
+            elif PASSES <= chunk < PASSES + PASSES * PASSES:
+                prepare_w2((chunk - PASSES) % PASSES, (chunk - PASSES) // PASSES)
 
-        turn_codes = keep.tile([P, 5 * PASS], U32, name="turn_codes", tag="turn", align_bytes=64)
+        turn_codes = keep.tile([P, (1 + PASSES * PASSES) * PASS], U32, name="turn_codes", tag="turn", align_bytes=64)
+        w2_q = {}
 
         def quantise_w2(c):
-            for b in range(2):
-                first = (1 + 2 * c + b) * PASS
+            for b in range(PASSES):
+                first = (1 + PASSES * c + b) * PASS
                 w2_q[b, c] = turn_codes[:, first : first + PASS], held([P, PASS], U8, f"w2_{b}{c}_sc")
                 quantise(w2_q[b, c][0], w2_q[b, c][1][:], w2_grouped[b, c][:])
 
@@ -273,12 +304,12 @@ def tile_list_sleep_episode_stager_kernel(
         quantise(z_q[1], z_sc[1][:], z[1][:])
         quantise_w2(1)
 
-        out_rows = out.rearrange("(b g t i) j -> b t g i j", b=2, t=PACK, i=8)
+        out_rows = out.rearrange("(c g t e) j -> c t g e j", c=PASSES, t=PACK, e=RUN)
 
         def second_stage(i):
             c, t = divmod(i, PACK)
             acc = psum.tile([P, BANK], F32, name="acc")
-            for b in range(2):
+            for b in range(PASSES):
                 codes, scales = w2_q[b, c]
                 nc.tensor.matmul_mx(
                     out=acc[:],
@@ -287,35 +318,35 @@ def tile_list_sleep_episode_stager_kernel(
                     rhs=z_q[b].bitcast(FP8X4),
                     rhs_scale=z_sc[b][:],
                     start=(b == 0),
-                    stop=(b == 1),
+                    stop=(b == PASSES - 1),
                 )
-            nc.scalar.copy(out=ya[i % 4][:, 0:E], in_=acc[:])
+            nc.scalar.copy(out=ya[i % WINDOWS][:, 0:E], in_=acc[:])
 
         def fetch_back(i):
-            yr = ring.tile([P, S], F32, name="yr", bufs=4)
-            nc.vector.tensor_copy(out=yr[:], in_=ya[i % 4][:].indirect(pos3_t[:]))
+            yr = ring.tile([P, S], F32, name="yr", bufs=FETCH_BUFS)
+            nc.vector.tensor_copy(out=yr[:], in_=ya[i % WINDOWS][:].indirect(pos3_t[:]))
             return yr
 
         def pieces(i):
-            width = BANK if i == TILES - 1 else S
+            width = S // 2 if i == TILES - 1 else S
             return [slice(first, first + width) for first in range(0, S, width)]
 
         def apply_gate(i, yr):
-            gate = ring.tile([P, S], F32, name="gate", bufs=3)
-            gated = ring.tile([P, S], F32, name="gated", bufs=3)
-            engine = nc.vector if i >= TILES - 2 else nc.gpsimd
+            gate = ring.tile([P, S], F32, name="gate", bufs=GATE_BUFS)
+            product = ring.tile([P, S], F32, name="gated", bufs=GATE_BUFS)
+            engine = nc.gpsimd if i < GPSIMD_GATES else nc.vector
             for cols in pieces(i):
                 nc.scalar.activation(out=gate[:, cols], in_=yr[:, cols], func=ACT.Sigmoid)
             for cols in pieces(i):
-                engine.tensor_tensor(out=gated[:, cols], in0=h[i][:, cols], in1=gate[:, cols], op=ALU.mult)
-            return gated
+                engine.tensor_tensor(out=product[:, cols], in0=h[i][:, cols], in1=gate[:, cols], op=ALU.mult)
+            return product
 
-        def finish(i, yr, gated):
+        def finish(i, yr, product):
             c, t = divmod(i, PACK)
             for cols in pieces(i):
                 nc.vector.scalar_tensor_tensor(
                     out=h[i][:, cols],
-                    in0=gated[:, cols],
+                    in0=product[:, cols],
                     scalar=gains[:, TILES + i : TILES + i + 1],
                     in1=yr[:, cols],
                     op0=ALU.mult,
@@ -323,15 +354,16 @@ def tile_list_sleep_episode_stager_kernel(
                 )
                 nc.sync.dma_start(out=out_rows[c, t][:, :, cols], in_=h[i][:, cols])
 
-        fetched, gated = {}, {}
-        for n in range(4):
+        lag = FETCH_BUFS - 1
+        fetched, products = {}, {}
+        for n in range(WINDOWS):
             second_stage(n)
-        for n in range(TILES + 3):
+        for n in range(TILES + lag):
             if n < TILES:
                 fetched[n] = fetch_back(n)
-            if n + 4 < TILES:
-                second_stage(n + 4)
-            if n >= 3:
-                finish(n - 3, fetched[n - 3], gated[n - 3])
+            if n + WINDOWS < TILES:
+                second_stage(n + WINDOWS)
+            if n >= lag:
+                finish(n - lag, fetched[n - lag], products[n - lag])
             if n < TILES:
-                gated[n] = apply_gate(n, fetched[n])
+                products[n] = apply_gate(n, fetched[n])

from contextlib import ExitStack

import concourse.mybir as mybir
from concourse.masks import make_identity

K, T, S, E, H = 1024, 2048, 1024, 512, 1024
FLOPS = 2 * (2 * K * H * S + H * H * E)

F32 = mybir.dt.float32
BF16 = mybir.dt.bfloat16
I32 = mybir.dt.int32
U32 = mybir.dt.uint32
U16 = mybir.dt.uint16
U8 = mybir.dt.uint8
FP8X4 = mybir.dt.float8_e4m3fn_x4
FP4X4 = mybir.dt.float4_e2m1fn_x4
ALU = mybir.AluOpType
ACT = mybir.ActivationFunctionType

P = 128
PACK = 4
PASS = P * PACK
BANK = 512
PASSES = K // PASS
TILES = H // P
HALVES = S // BANK
BLOCKS = P // 8
RUN = 8
QUADRANTS = 4

WINDOWS = 4
RAW_BUFS = 2
STAGING_BUFS = 4
FETCH_BUFS = 4
GATE_BUFS = 3
UNSKEWED = 2
CAST_LAG = 2
GPSIMD_ADDS = 4
GPSIMD_SCALES = 6
GPSIMD_GATES = 6


def tile_list_sleep_episode_stager_kernel(
    tc, tab_words, tab_scales, offs, pos1, pos2, pos3, w1, w4_words, w4_scales, w2, gp, gs, out
):
    nc = tc.nc
    with ExitStack() as ctx:
        keep = ctx.enter_context(tc.tile_pool(name="keep", bufs=1))
        ring = ctx.enter_context(tc.tile_pool(name="ring", bufs=2))
        psum = ctx.enter_context(tc.psum_pool(name="psum", bufs=8))

        def held(shape, dtype, name):
            return keep.tile(shape, dtype, name=name, align_bytes=64)

        offs_t = held([P, S // 16], U16, "offs_t")
        pos1_t = held([P, E // 16], U16, "pos1_t")
        pos2_t = held([P, E // 16], U16, "pos2_t")
        pos3_t = held([P, S // 16], U16, "pos3_t")
        table = [held([P, T], U32, f"table{a}") for a in range(PASSES)]
        table_sc = held([P, T], U8, "table_sc")
        table_sc_rows = held([P, T], U8, "table_sc_rows")
        v = [[held([P, BANK], U32, f"v{a}{u}") for u in range(HALVES)] for a in range(PASSES)]
        v_sc = held([P, S], U8, "v_sc")
        v_sc1 = held([P, S], U8, "v_sc1")
        w4_raw = [held([P, PASSES * 2 * PASS], U8, f"w4_raw{b}") for b in range(PASSES)]
        w4 = [held([P, PASSES * 2 * PASS], U8, f"w4_{b}") for b in range(PASSES)]
        w4_sc_raw = held([P, PASSES * H], U8, "w4_sc_raw")
        w4_sc = held([P, PASSES * H], U8, "w4_sc")
        gains_rows = held([P, P], F32, "gains_rows")
        ident = held([P, P], F32, "ident")
        gains = held([P, 2 * TILES], F32, "gains")
        h = [held([P, S], F32, f"h{i}") for i in range(TILES)]
        ya = [held([P, E + S], F32, f"ya{i}") for i in range(WINDOWS)]
        z = [held([P, E * PACK], BF16, f"z{b}") for b in range(PASSES)]
        z_sc = [held([P, E], U8, f"z_sc{b}") for b in range(PASSES)]

        nc.vector.memset(w4_sc_raw[:].bitcast(I32), 0)
        nc.vector.memset(table_sc[:].bitcast(I32), 0)
        nc.vector.memset(v_sc1[:].bitcast(I32), 0)
        nc.gpsimd.memset(gains_rows[:], 0.0)
        make_identity(nc, ident[:])

        def load_table(a):
            nc.sync.dma_start(
                out=table[a][:].bitcast(I32), in_=tab_words[a].rearrange("p n i -> p (n i)").bitcast(I32)
            )

        def load_w1(a, b):
            raw = ring.tile([P, PACK, PASS], F32, name="raw", bufs=RAW_BUFS)
            rows = w1[a * PASS : (a + 1) * PASS, b * PASS : (b + 1) * PASS]
            nc.sync.dma_start(out=raw[:], in_=rows.rearrange("(p j) c -> p j c", j=PACK))
            return raw

        def load_w4(b):
            words = w4_words[:, :, 2 * b * PASS : 2 * (b + 1) * PASS].bitcast(I32)
            nc.sync.dma_start(
                out=w4_raw[b][:].bitcast(I32).rearrange("p (a c) -> p a c", a=PASSES),
                in_=words.rearrange("a p c -> p a c"),
            )

        def deal(dst, src, words, engine):
            engine.tensor_copy(
                out=dst[:].bitcast(I32).rearrange("p (s t g w) -> p s t g w", t=PACK, g=BLOCKS, w=words),
                in_=src[:].bitcast(I32).rearrange("p (s g t w) -> p s t g w", t=PACK, g=BLOCKS, w=words),
            )

        def load_w2(b, c):
            raw = ring.tile([P, PACK, PASS], F32, name="raw", bufs=RAW_BUFS)
            rows = w2[b * PASS : (b + 1) * PASS, c * PASS : (c + 1) * PASS]
            rows = rows.rearrange("(g t e) n -> t g e n", t=PACK, e=RUN)
            for t in range(PACK):
                nc.sync.dma_start(out=raw[:, t, :], in_=rows[t])
            return raw

        def regroup(raw, grouped, t):
            src = raw[:].rearrange("p j (g t u n) -> p t g u j n", t=PACK, u=2, n=4)
            dst = grouped[:].rearrange("p (t g u n j) -> p t g u j n", t=PACK, u=2, n=4, j=PACK)
            nc.scalar.copy(out=dst[:, t], in_=src[:, t])

        def staging():
            return ring.tile([P, PASS * PACK], BF16, name="grouped", bufs=STAGING_BUFS, align_bytes=64)

        def quantise(codes, scales, values):
            nc.vector.quantize_mx(out=codes.bitcast(FP8X4), scales=scales, in_=values)

        def quantise_w1(raw, a, b):
            grouped = staging()
            codes = held([P, PASS], U32, f"w1_{a}{b}_q")
            scales = held([P, PASS], U8, f"w1_{a}{b}_sc")
            for t in range(PACK):
                regroup(raw, grouped, t)
                if b == 0 and t == 0:
                    quantise(codes[:, 0:P], scales[:, 0:P], grouped[:, 0:PASS])
            done = P if b == 0 else 0
            quantise(codes[:, done:], scales[:, done:], grouped[:, done * PACK :])
            return codes, scales

        nc.sync.dma_start(offs_t[:], offs)
        for q in range(QUADRANTS):
            nc.sync.dma_start(
                out=table_sc_rows[32 * q : 32 * q + 8, :].bitcast(I32),
                in_=tab_scales[:, 4 * q : 4 * q + 4, :].bitcast(I32),
            )
        load_table(0)
        w1_first = load_w1(0, 0)
        load_table(1)
        load_w4(0)
        for q in range(QUADRANTS):
            nc.sync.dma_start(
                out=w4_sc_raw[32 * q : 32 * q + 4, :].bitcast(I32).rearrange("r (a c) -> r a c", a=PASSES),
                in_=w4_scales[:, 4 * q : 4 * q + 4, :].bitcast(I32).rearrange("a r c -> r a c"),
            )
        w1_second = load_w1(1, 0)
        nc.sync.dma_start(pos1_t[:], pos1)
        nc.sync.dma_start(pos2_t[:], pos2)
        for n, vec in enumerate((gp, gs)):
            for b in range(PASSES):
                row = n * TILES + b * PACK
                nc.sync.dma_start(
                    out=gains_rows[row : row + PACK, :].rearrange("t (g e) -> t g e", e=RUN),
                    in_=vec[b * PASS : (b + 1) * PASS].rearrange("(g t e) -> t g e", t=PACK, e=RUN),
                )
        nc.sync.dma_start(pos3_t[:], pos3)
        load_w4(1)

        for q in range(QUADRANTS):
            rows = slice(32 * q, 32 * q + 8)
            nc.vector.tensor_copy(out=table_sc[rows, :].bitcast(I32), in_=table_sc_rows[rows, :].bitcast(I32))
        nc.vector.tensor_copy(out=v_sc[:], in_=table_sc[:].indirect(offs_t[:]))
        nc.gpsimd.dma_start(out=v_sc1[0:100, :].bitcast(I32), in_=v_sc[4:104, :].bitcast(I32))

        def gather_table(a):
            for u in range(HALVES):
                offsets = offs_t[:, u * BANK // 16 : (u + 1) * BANK // 16]
                nc.vector.tensor_copy(out=v[a][u][:], in_=table[a][:].indirect(offsets))

        w1_q = {}
        gather_table(0)
        w1_q[0, 0] = quantise_w1(w1_first, 0, 0)
        gather_table(1)
        deal(w4_sc, w4_sc_raw, RUN // 4, nc.vector)
        deal(w4[0], w4_raw[0], 2 * RUN // 4, nc.vector)
        w1_q[1, 0] = quantise_w1(w1_second, 1, 0)
        deal(w4[1], w4_raw[1], 2 * RUN // 4, nc.gpsimd)

        def turn_gains():
            turned = psum.tile([P, BANK], F32, name="acc")
            nc.tensor.transpose(turned[:, 0:P], gains_rows[:], ident[:])
            nc.scalar.copy(out=gains[:], in_=turned[:, 0 : 2 * TILES])

        def first_stage(i, u):
            b, t = divmod(i, PACK)
            cols = slice(u * BANK, (u + 1) * BANK)
            acc_a = psum.tile([P, BANK], F32, name="acc")
            for a in range(PASSES):
                codes, scales = w1_q[a, b]
                nc.tensor.matmul_mx(
                    out=acc_a[:],
                    lhsT=codes[:, t * P : (t + 1) * P].bitcast(FP8X4),
                    lhsT_scale=scales[:, t * P : (t + 1) * P],
                    rhs=v[a][u][:].bitcast(FP8X4),
                    rhs_scale=v_sc[4 * a : P, cols],
                    start=(a == 0),
                    stop=(a == PASSES - 1),
                )
            acc_b = psum.tile([P, BANK], F32, name="acc")
            for a in range(PASSES):
                scale_col = a * H + i * P
                word_col = a * PASS + t * P
                nc.tensor.matmul_mx(
                    out=acc_b[:],
                    lhsT=w4[b][:, 2 * word_col : 2 * (word_col + P)].bitcast(FP4X4),
                    lhsT_scale=w4_sc[:, scale_col : scale_col + P],
                    rhs=v[a][u][:].bitcast(FP8X4),
                    rhs_scale=(v_sc, v_sc1)[a][:, cols],
                    start=(a == 0),
                    stop=(a == PASSES - 1),
                )
            a_sb = ya[i % WINDOWS][:, E + u * BANK : E + (u + 1) * BANK]
            nc.scalar.copy(out=a_sb, in_=acc_a[:])
            nc.vector.tensor_tensor(out=h[i][:, cols], in0=acc_b[:], in1=a_sb, op=ALU.max)

        last_picked = keep.tile([P, E], F32, name="last_picked", tag="turn", align_bytes=64)
        early = [ring.tile([P, E], F32, name="yr", bufs=FETCH_BUFS) for n in range(2 * UNSKEWED)]

        def picked(i):
            if i < UNSKEWED:
                return early[2 * i][:]
            return last_picked[:] if i == TILES - 1 else ya[(i + 1) % WINDOWS][:, E + BANK :]

        def paired(i):
            return early[2 * i + 1][:] if i < UNSKEWED else ya[(i + 2) % WINDOWS][:, E : E + BANK]

        def pick_first(i):
            nc.vector.tensor_copy(out=picked(i), in_=h[i][:].indirect(pos1_t[:]))

        def join_pair(i):
            pair = paired(i)
            if i >= GPSIMD_ADDS:
                nc.vector.tensor_tensor(out=pair, in0=h[i][:].indirect(pos2_t[:]), in1=picked(i), op=ALU.add)
            else:
                nc.vector.tensor_copy(out=pair, in_=h[i][:].indirect(pos2_t[:]))
                nc.gpsimd.tensor_tensor(out=pair, in0=pair, in1=picked(i), op=ALU.add)

        def scale_pair(i):
            b, t = divmod(i, PACK)
            place = z[b][:].rearrange("p (m t) -> p t m", t=PACK)[:, t, :]
            pair = paired(i)
            if i < GPSIMD_SCALES:
                nc.gpsimd.tensor_scalar(
                    out=place, in0=pair, scalar1=gains[:, i : i + 1], scalar2=0.0, op0=ALU.mult, op1=ALU.add
                )
            else:
                nc.scalar.activation(out=place, in_=pair, func=ACT.Copy, scale=gains[:, i : i + 1])

        w2_grouped = {}

        def prepare_w1(a):
            w1_q[a, 1] = quantise_w1(load_w1(a, 1), a, 1)

        def prepare_w2(b, c):
            raw = load_w2(b, c)
            w2_grouped[b, c] = staging()
            for t in range(PACK):
                regroup(raw, w2_grouped[b, c], t)

        for i in range(TILES + 2):
            if i < TILES:
                first_stage(i, 0)
            if i - 2 >= UNSKEWED:
                join_pair(i - 2)
            if i < TILES:
                first_stage(i, 1)
            if i == UNSKEWED - 1:
                turn_gains()
                scale_pair(i - 1)
            if i - 2 >= UNSKEWED:
                scale_pair(i - 2)
            if i < UNSKEWED:
                pick_first(i)
                join_pair(i)
            if i == UNSKEWED - 1:
                scale_pair(i)
            if UNSKEWED <= i - 1 < TILES:
                pick_first(i - 1)
            chunk = i - CAST_LAG
            if 0 <= chunk < PASSES:
                prepare_w1(chunk)
            elif PASSES <= chunk < PASSES + PASSES * PASSES:
                prepare_w2((chunk - PASSES) % PASSES, (chunk - PASSES) // PASSES)

        turn_codes = keep.tile([P, (1 + PASSES * PASSES) * PASS], U32, name="turn_codes", tag="turn", align_bytes=64)
        w2_q = {}

        def quantise_w2(c):
            for b in range(PASSES):
                first = (1 + PASSES * c + b) * PASS
                w2_q[b, c] = turn_codes[:, first : first + PASS], held([P, PASS], U8, f"w2_{b}{c}_sc")
                quantise(w2_q[b, c][0], w2_q[b, c][1][:], w2_grouped[b, c][:])

        z_q = [turn_codes[:, 0:E], held([P, E], U32, "z_q1")[:]]
        quantise(z_q[0], z_sc[0][:], z[0][:])
        quantise_w2(0)
        quantise(z_q[1], z_sc[1][:], z[1][:])
        quantise_w2(1)

        out_rows = out.rearrange("(c g t e) j -> c t g e j", c=PASSES, t=PACK, e=RUN)

        def second_stage(i):
            c, t = divmod(i, PACK)
            acc = psum.tile([P, BANK], F32, name="acc")
            for b in range(PASSES):
                codes, scales = w2_q[b, c]
                nc.tensor.matmul_mx(
                    out=acc[:],
                    lhsT=codes[:, t * P : (t + 1) * P].bitcast(FP8X4),
                    lhsT_scale=scales[:, t * P : (t + 1) * P],
                    rhs=z_q[b].bitcast(FP8X4),
                    rhs_scale=z_sc[b][:],
                    start=(b == 0),
                    stop=(b == PASSES - 1),
                )
            nc.scalar.copy(out=ya[i % WINDOWS][:, 0:E], in_=acc[:])

        def fetch_back(i):
            yr = ring.tile([P, S], F32, name="yr", bufs=FETCH_BUFS)
            nc.vector.tensor_copy(out=yr[:], in_=ya[i % WINDOWS][:].indirect(pos3_t[:]))
            return yr

        def pieces(i):
            width = S // 2 if i == TILES - 1 else S
            return [slice(first, first + width) for first in range(0, S, width)]

        def apply_gate(i, yr):
            gate = ring.tile([P, S], F32, name="gate", bufs=GATE_BUFS)
            product = ring.tile([P, S], F32, name="gated", bufs=GATE_BUFS)
            engine = nc.gpsimd if i < GPSIMD_GATES else nc.vector
            for cols in pieces(i):
                nc.scalar.activation(out=gate[:, cols], in_=yr[:, cols], func=ACT.Sigmoid)
            for cols in pieces(i):
                engine.tensor_tensor(out=product[:, cols], in0=h[i][:, cols], in1=gate[:, cols], op=ALU.mult)
            return product

        def finish(i, yr, product):
            c, t = divmod(i, PACK)
            for cols in pieces(i):
                nc.vector.scalar_tensor_tensor(
                    out=h[i][:, cols],
                    in0=product[:, cols],
                    scalar=gains[:, TILES + i : TILES + i + 1],
                    in1=yr[:, cols],
                    op0=ALU.mult,
                    op1=ALU.add,
                )
                nc.sync.dma_start(out=out_rows[c, t][:, :, cols], in_=h[i][:, cols])

        lag = FETCH_BUFS - 1
        fetched, products = {}, {}
        for n in range(WINDOWS):
            second_stage(n)
        for n in range(TILES + lag):
            if n < TILES:
                fetched[n] = fetch_back(n)
            if n + WINDOWS < TILES:
                second_stage(n + WINDOWS)
            if n >= lag:
                finish(n - lag, fetched[n - lag], products[n - lag])
            if n < TILES:
                products[n] = apply_gate(n, fetched[n])
